import numpy as np
import ml_dtypes


def mxq(x, axis, fmt="e4m3"):
    dtype, down = {"e4m3": (ml_dtypes.float8_e4m3fn, 7), "e5m2": (ml_dtypes.float8_e5m2, 14)}[fmt]
    v = np.moveaxis(np.asarray(x, np.float32).astype(ml_dtypes.bfloat16).astype(np.float64), axis, -1)
    blocks = v.reshape(v.shape[:-1] + (-1, 32))
    amax = np.abs(blocks).max(-1, keepdims=True)
    byte = np.maximum(np.where(amax > 0, np.frexp(amax)[1] - 1 + 127, 0) - down, 1)
    scale = np.exp2(byte - 127.0)
    codes = (blocks / scale).astype(np.float32).astype(dtype).astype(np.float64)
    return np.moveaxis((codes * scale).reshape(v.shape), -1, axis)


WIDE = False


def mx_kscale(k):
    if not WIDE:
        return np.ones(k)
    levels = np.array([24, -24, 12, -12, 0])
    if k % 512:
        return np.exp2(np.random.permutation(np.resize(levels, k // 32))).repeat(32)
    a = np.empty((k // 512, 16))
    for p in range(k // 512):
        a[p, :8] = np.random.permutation(np.resize(levels, 8))
        for g in range(8):
            far = levels[np.abs(levels - a[p, g]) >= 10]
            a[p, g + 8] = far[np.random.randint(len(far))]
    return np.exp2(a.ravel()).repeat(32)


def f64(x):
    return np.asarray(x).astype(np.float64)


def striped8(idx):
    return np.concatenate([v.reshape(-1, 16).T for v in idx]).astype(np.uint16)


def unstriped8(offs):
    return np.stack([offs[16 * g:16 * g + 16].T.reshape(-1) for g in range(8)]).astype(np.int64)


def planes(y):
    n, m = y.shape
    v = y.astype(np.float32).astype(ml_dtypes.bfloat16).astype(np.float64).reshape(n // 32, 32, m)
    top = np.abs(v).max(1)
    byte = np.clip(np.where(top > 0, np.frexp(top)[1] - 1 + 127 - 7, 1), 1, 254)
    codes = (v * np.exp2(127.0 - byte)[:, None, :]).reshape(n, m).astype(np.float32).astype(ml_dtypes.float8_e4m3fn).view(np.uint8)
    words = codes.reshape(n // 512, 128, 4, m).transpose(0, 1, 3, 2)
    return np.ascontiguousarray(words), np.ascontiguousarray(byte.astype(np.uint8).reshape(n // 512, 16, m))


K, N, T, J = 512, 512, 2048, 512


def setup_inputs():
    n = np.random.standard_normal
    s = mx_kscale(K)[:, None]
    return {
        "xT": (n((K, T)) * s).astype(np.float32),
        "wgt": np.repeat(np.random.uniform(0.5, 2.0, (8, 3 * J)), 16, axis=0).astype(np.float32),
        "w": (n((K, N)) / np.sqrt(K) / s).astype(np.float32),
        "offs": striped8(np.stack([np.concatenate([np.random.permutation(T)[:J] for _ in range(3)]) for _ in range(8)])),
    }


def reference(xT, wgt, w, offs):
    idx = unstriped8(offs)
    rows = np.arange(K)
    xg = f64(wgt)[rows // 4 % 128] * f64(xT)[rows[:, None], idx[rows % 512 // 64]]
    xT_ = mxq(xg, 0, "e4m3").reshape(K, 3, J)
    w_ = mxq(f64(w), 0, "e4m3")
    a0 = w_.T @ xT_[:, 0]
    a1 = w_.T @ xT_[:, 1]
    a2 = w_.T @ xT_[:, 2]
    out_0 = np.maximum(np.maximum(a0, a1), a2)
    return (out_0,) + planes(out_0)

@@ -1,0 +1,174 @@
+from contextlib import ExitStack
+
+import concourse.mybir as mybir
+
+K, N, T, J, PICKS = 512, 512, 2048, 512, 3
+FLOPS = 2 * K * N * J * PICKS
+
+F32 = mybir.dt.float32
+BF16 = mybir.dt.bfloat16
+U32 = mybir.dt.uint32
+I32 = mybir.dt.int32
+U16 = mybir.dt.uint16
+U8 = mybir.dt.uint8
+FP8X4 = mybir.dt.float8_e4m3fn_x4
+MULT = mybir.AluOpType.mult
+MAX = mybir.AluOpType.max
+
+P = 128
+PACK = 4
+BANK = 512
+HALF = J // 2
+ROW = J + HALF
+WGT_AT = 2 * ROW + HALF
+
+
+def tile_list_max_noneP_kernel(tc, xT, wgt, w, offs, out_0, out_1, out_2):
+    nc = tc.nc
+    with ExitStack() as ctx:
+        keep = ctx.enter_context(tc.tile_pool(name="keep", bufs=1))
+        psum = ctx.enter_context(tc.psum_pool(name="psum", bufs=1))
+
+        offsets = keep.tile([P, PICKS * J // 16], U16, name="offsets")
+        planes = [keep.tile([P, T], F32, name=f"plane{t}") for t in range(PACK)]
+        picked = [keep.tile([P, PACK * ROW], F32, name=f"picked{c}") for c in range(PICKS)]
+        grouped = [keep.tile([P, J * PACK], BF16, name=f"grouped{c}", align_bytes=64) for c in range(PICKS)]
+        codes = [keep.tile([P, J], U32, name=f"codes{c}", align_bytes=64) for c in range(PICKS)]
+        scales = [keep.tile([P, J], U8, name=f"scales{c}", align_bytes=64) for c in range(PICKS)]
+        w_raw = keep.tile([P, PACK, N], F32, name="w_raw")
+        w_grouped = keep.tile([P, N * PACK], BF16, name="w_grouped", align_bytes=64)
+        w_codes = keep.tile([P, N], U32, name="w_codes", align_bytes=64)
+        w_scales = keep.tile([P, N], U8, name="w_scales", align_bytes=64)
+        y_codes = keep.tile([P, J], U32, name="y_codes", align_bytes=64)
+        y_scales = keep.tile([P, J], U8, name="y_scales", align_bytes=64)
+        x_rows = xT.rearrange("(p t) j -> p t j", t=PACK)
+        out_rows = out_0.rearrange("(p t) j -> p t j", t=PACK)
+        out_words = out_1[0].rearrange("p j t -> p (j t)").bitcast(I32)
+
+        nc.sync.dma_start(out=planes[0][:], in_=x_rows[:, 0, :])
+        nc.sync.dma_start(offsets[:], offs)
+        for c in range(PICKS):
+            nc.sync.dma_start(out=picked[c][:, WGT_AT : WGT_AT + J], in_=wgt[:, c * J : (c + 1) * J])
+        nc.sync.dma_start(out=planes[1][:], in_=x_rows[:, 1, :])
+        nc.sync.dma_start(out=w_raw[:], in_=w.rearrange("(p t) n -> p t n", t=PACK))
+        nc.sync.dma_start(out=planes[2][:], in_=x_rows[:, 2, :])
+        nc.sync.dma_start(out=planes[3][:], in_=x_rows[:, 3, :])
+
+        def gather(c, t, a, n):
+            nc.vector.tensor_tensor(
+                picked[c][:, t * ROW + a : t * ROW + a + n],
+                planes[t][:].indirect(offsets[:, (c * J + a) // 16 : (c * J + a + n) // 16]),
+                picked[c][:, WGT_AT + a : WGT_AT + a + n],
+                MULT,
+            )
+
+        def interleave(dst, src):
+            nc.scalar.copy(
+                out=dst.rearrange("p (c i) t -> p c t i", i=4),
+                in_=src.rearrange("p t (c i) -> p c t i", i=4),
+            )
+
+        def group(c, t0, t1, a, n):
+            interleave(
+                grouped[c][:].rearrange("p (j t) -> p j t", t=PACK)[:, a : a + n, t0:t1],
+                picked[c][:].rearrange("p (t j) -> p t j", t=PACK)[:, t0:t1, a : a + n],
+            )
+
+        def quantize(cod, sca, src):
+            nc.vector.quantize_mx(out=cod.bitcast(FP8X4), scales=sca, in_=src)
+
+        def project(c, a, n, banks):
+            quantize(codes[c][:, a : a + n], scales[c][:, a : a + n], grouped[c][:, PACK * a : PACK * (a + n)])
+            per = BANK // n
+            sums = []
+            for s, bank in enumerate(banks):
+                acc = psum.tile([P, per, n], F32, name=f"sum_{c}_{a}_{s}", tag=f"bank{bank}")
+                for u in range(per):
+                    cols = slice(P * (s * per + u), P * (s * per + u + 1))
+                    nc.tensor.matmul_mx(
+                        out=acc[:, u, :],
+                        lhsT=w_codes[:, cols].bitcast(FP8X4),
+                        lhsT_scale=w_scales[:, cols],
+                        rhs=codes[c][:, a : a + n].bitcast(FP8X4),
+                        rhs_scale=scales[c][:, a : a + n],
+                        start=True,
+                        stop=True,
+                    )
+                sums.append(acc)
+            return sums
+
+        def evacuate(sums, name):
+            tiles = []
+            for s, acc in enumerate(sums):
+                tile = keep.tile([P, 2, HALF], F32, name=f"{name}{s}")
+                nc.scalar.copy(out=tile[:], in_=acc[:])
+                tiles.append(tile)
+            return tiles
+
+        def pool_two(best, sums, firsts):
+            for s, acc in enumerate(sums):
+                nc.vector.tensor_tensor(best[:, 2 * s : 2 * s + 2, :], acc[:], firsts[s][:], MAX)
+
+        def pool_last(sums, best, a, n):
+            per = BANK // n
+            y = keep.tile([P, PACK, n], F32, name=f"y{a}")
+            for s, acc in enumerate(sums):
+                nc.vector.tensor_tensor(y[:, s * per : (s + 1) * per, :], acc[:], best[:, s * per : (s + 1) * per, a % HALF : a % HALF + n], MAX)
+            nc.sync.dma_start(out=out_rows[:, :, a : a + n], in_=y[:])
+            y_grouped = keep.tile([P, n, PACK], BF16, name=f"y_grouped{a}", align_bytes=64)
+            interleave(y_grouped[:], y[:])
+            return y_grouped
+
+        def quantize_y(y_grouped, a, n):
+            quantize(y_codes[:, a : a + n], y_scales[:, a : a + n], y_grouped[:].rearrange("p j t -> p (j t)"))
+
+        for c in range(PICKS):
+            gather(c, 0, 0, J)
+        gather(0, 1, 0, J)
+        group(0, 0, 2, 0, J)
+        nc.scalar.copy(
+            out=w_grouped[:].rearrange("p (t m k) -> p m t k", t=PACK, k=PACK),
+            in_=w_raw[:].rearrange("p k (m t) -> p m t k", t=PACK),
+        )
+        gather(1, 1, 0, J)
+        group(1, 0, 2, 0, J)
+        gather(2, 1, 0, J)
+        for c in range(PICKS):
+            gather(c, 2, 0, HALF)
+        quantize(w_codes[:], w_scales[:], w_grouped[:])
+        for c in range(PICKS):
+            gather(c, 3, 0, HALF)
+            group(c, 2 if c < 2 else 0, PACK, 0, HALF)
+
+        best = [keep.tile([P, PACK, HALF], F32, name=f"best{h}") for h in range(2)]
+        sums0 = project(0, 0, HALF, (0, 1))
+        first_a = evacuate(sums0, "first_a")
+        sums1 = project(1, 0, HALF, (2, 3))
+        for t in (2, 3):
+            gather(0, t, HALF, HALF)
+        group(0, 2, PACK, HALF, HALF)
+        sums2 = project(2, 0, HALF, (4, 5))
+        for t in (2, 3):
+            gather(1, t, HALF, HALF)
+        group(1, 2, PACK, HALF, HALF)
+        sums0b = project(0, HALF, HALF, (6, 7))
+        first_b = evacuate(sums0b, "first_b")
+        for a in (HALF, HALF + P):
+            for t in (2, 3):
+                gather(2, t, a, P)
+            group(2, 0, PACK, a, P)
+        pool_two(best[0], sums1, first_a)
+        sums1b = project(1, HALF, HALF, (0, 1))
+        y_a = pool_last(sums2, best[0], 0, HALF)
+        sums2b = [project(2, a, P, (bank,)) for a, bank in ((HALF, 2), (HALF + P, 3))]
+        pool_two(best[1], sums1b, first_b)
+        y_b1 = pool_last(sums2b[0], best[1], HALF, P)
+        quantize_y(y_a, 0, HALF)
+        nc.sync.dma_start(out=out_words[:, 0:HALF], in_=y_codes[:, 0:HALF].bitcast(I32))
+        y_b2 = pool_last(sums2b[1], best[1], HALF + P, P)
+        quantize_y(y_b1, HALF, P)
+        quantize_y(y_b2, HALF + P, P)
+        nc.scalar.dma_start(out=out_words[:, HALF:J], in_=y_codes[:, HALF:J].bitcast(I32))
+        for q in range(4):
+            eng = nc.sync if q % 2 == 0 else nc.scalar
+            eng.dma_start(out=out_2[0, 4 * q : 4 * q + 4, :].bitcast(I32), in_=y_scales[32 * q : 32 * q + 4, :].bitcast(I32))

@@ -19,8 +19,6 @@ P = 128
 PACK = 4
 BANK = 512
 HALF = J // 2
-ROW = J + HALF
-WGT_AT = 2 * ROW + HALF
 
 
 def tile_list_max_noneP_kernel(tc, xT, wgt, w, offs, out_0, out_1, out_2):
@@ -31,13 +29,16 @@ def tile_list_max_noneP_kernel(tc, xT, wgt, w, offs, out_0, out_1, out_2):
 
         offsets = keep.tile([P, PICKS * J // 16], U16, name="offsets")
         planes = [keep.tile([P, T], F32, name=f"plane{t}") for t in range(PACK)]
-        picked = [keep.tile([P, PACK * ROW], F32, name=f"picked{c}") for c in range(PICKS)]
-        grouped = [keep.tile([P, J * PACK], BF16, name=f"grouped{c}", align_bytes=64) for c in range(PICKS)]
+        factors = keep.tile([P, PICKS * J], F32, name="factors")
+        early = [keep.tile([P, 2 * J], F32, name=f"early{c}") for c in range(2)]
+        late_a = [keep.tile([P, (2 if c < 2 else PACK) * HALF], F32, name=f"late_a{c}", tag=f"late_a{c}", align_bytes=64) for c in range(PICKS)]
+        late_b = [keep.tile([P, (3, 2, 4)[c] * HALF], F32, name=f"late_b{c}", align_bytes=64) for c in range(PICKS)]
+        grouped_a = [late_b[c][:, (1, 0, 2)[c] * HALF :].bitcast(BF16) for c in range(PICKS)]
+        grouped_b = [keep.tile([P, HALF * PACK], BF16, name=f"grouped_b{c}", align_bytes=64) for c in range(PICKS)]
         codes = [keep.tile([P, J], U32, name=f"codes{c}", align_bytes=64) for c in range(PICKS)]
         scales = [keep.tile([P, J], U8, name=f"scales{c}", align_bytes=64) for c in range(PICKS)]
         w_raw = keep.tile([P, PACK, N], F32, name="w_raw")
         w_grouped = keep.tile([P, N * PACK], BF16, name="w_grouped", align_bytes=64)
-        w_codes = keep.tile([P, N], U32, name="w_codes", align_bytes=64)
         w_scales = keep.tile([P, N], U8, name="w_scales", align_bytes=64)
         y_codes = keep.tile([P, J], U32, name="y_codes", align_bytes=64)
         y_scales = keep.tile([P, J], U8, name="y_scales", align_bytes=64)
@@ -47,18 +48,29 @@ def tile_list_max_noneP_kernel(tc, xT, wgt, w, offs, out_0, out_1, out_2):
 
         nc.sync.dma_start(out=planes[0][:], in_=x_rows[:, 0, :])
         nc.sync.dma_start(offsets[:], offs)
-        for c in range(PICKS):
-            nc.sync.dma_start(out=picked[c][:, WGT_AT : WGT_AT + J], in_=wgt[:, c * J : (c + 1) * J])
+        for a, b in ((0, P), (P, J), (J, PICKS * J)):
+            nc.sync.dma_start(out=factors[:, a:b], in_=wgt[:, a:b])
         nc.sync.dma_start(out=planes[1][:], in_=x_rows[:, 1, :])
-        nc.sync.dma_start(out=w_raw[:], in_=w.rearrange("(p t) n -> p t n", t=PACK))
         nc.sync.dma_start(out=planes[2][:], in_=x_rows[:, 2, :])
+        nc.sync.dma_start(out=w_raw[:], in_=w.rearrange("(p t) n -> p t n", t=PACK))
         nc.sync.dma_start(out=planes[3][:], in_=x_rows[:, 3, :])
+
+        def picked(c, t0, t1, a, n):
+            if c < 2 and t0 < 2:
+                return early[c][:].rearrange("p (t j) -> p t j", j=J)[:, t0:t1, a : a + n]
+            skip = 2 if c < 2 else 0
+            tile = late_a[c] if a < HALF else late_b[c]
+            return tile[:].rearrange("p (t j) -> p t j", j=HALF)[:, t0 - skip : t1 - skip, a % HALF : a % HALF + n]
+
+        def grouped(c, a, n):
+            half = grouped_a[c] if a < HALF else grouped_b[c][:]
+            return half[:, PACK * (a % HALF) : PACK * (a % HALF + n)]
 
         def gather(c, t, a, n):
             nc.vector.tensor_tensor(
-                picked[c][:, t * ROW + a : t * ROW + a + n],
+                picked(c, t, t + 1, a, n)[:, 0, :],
                 planes[t][:].indirect(offsets[:, (c * J + a) // 16 : (c * J + a + n) // 16]),
-                picked[c][:, WGT_AT + a : WGT_AT + a + n],
+                factors[:, c * J + a : c * J + a + n],
                 MULT,
             )
 
@@ -70,15 +82,17 @@ def tile_list_max_noneP_kernel(tc, xT, wgt, w, offs, out_0, out_1, out_2):
 
         def group(c, t0, t1, a, n):
             interleave(
-                grouped[c][:].rearrange("p (j t) -> p j t", t=PACK)[:, a : a + n, t0:t1],
-                picked[c][:].rearrange("p (t j) -> p t j", t=PACK)[:, t0:t1, a : a + n],
+                grouped(c, a, n).rearrange("p (j t) -> p j t", t=PACK)[:, :, t0:t1],
+                picked(c, t0, t1, a, n),
             )
 
         def quantize(cod, sca, src):
             nc.vector.quantize_mx(out=cod.bitcast(FP8X4), scales=sca, in_=src)
 
+        def quantize_x(c, a, n):
+            quantize(codes[c][:, a : a + n], scales[c][:, a : a + n], grouped(c, a, n))
+
         def project(c, a, n, banks):
-            quantize(codes[c][:, a : a + n], scales[c][:, a : a + n], grouped[c][:, PACK * a : PACK * (a + n)])
             per = BANK // n
             sums = []
             for s, bank in enumerate(banks):
@@ -122,35 +136,44 @@ def tile_list_max_noneP_kernel(tc, xT, wgt, w, offs, out_0, out_1, out_2):
         def quantize_y(y_grouped, a, n):
             quantize(y_codes[:, a : a + n], y_scales[:, a : a + n], y_grouped[:].rearrange("p j t -> p (j t)"))
 
-        for c in range(PICKS):
-            gather(c, 0, 0, J)
-        gather(0, 1, 0, J)
-        group(0, 0, 2, 0, J)
+        gather(0, 0, 0, P)
+        gather(0, 0, P, J - P)
+        gather(1, 0, 0, J)
+        gather(2, 0, 0, HALF)
+        gather(2, 0, HALF, HALF)
+        for c in range(2):
+            gather(c, 1, 0, J)
+            group(c, 0, 2, 0, HALF)
+            group(c, 0, 2, HALF, HALF)
+        gather(2, 1, 0, HALF)
+        gather(2, 1, HALF, HALF)
         nc.scalar.copy(
-            out=w_grouped[:].rearrange("p (t m k) -> p m t k", t=PACK, k=PACK),
-            in_=w_raw[:].rearrange("p k (m t) -> p m t k", t=PACK),
+            out=w_grouped[:].rearrange("p (t m k) -> p m k t", t=PACK, k=PACK),
+            in_=w_raw[:].rearrange("p k (m t) -> p m k t", t=PACK),
         )
-        gather(1, 1, 0, J)
-        group(1, 0, 2, 0, J)
-        gather(2, 1, 0, J)
         for c in range(PICKS):
             gather(c, 2, 0, HALF)
-        quantize(w_codes[:], w_scales[:], w_grouped[:])
+        gather(0, 2, HALF, HALF)
         for c in range(PICKS):
             gather(c, 3, 0, HALF)
             group(c, 2 if c < 2 else 0, PACK, 0, HALF)
 
         best = [keep.tile([P, PACK, HALF], F32, name=f"best{h}") for h in range(2)]
+        quantize_x(0, 0, HALF)
+        w_codes = keep.tile([P, N], U32, name="w_codes", tag="late_a0", align_bytes=64)
+        quantize(w_codes[:], w_scales[:], w_grouped[:])
         sums0 = project(0, 0, HALF, (0, 1))
         first_a = evacuate(sums0, "first_a")
+        quantize_x(1, 0, HALF)
         sums1 = project(1, 0, HALF, (2, 3))
-        for t in (2, 3):
-            gather(0, t, HALF, HALF)
+        gather(0, 3, HALF, HALF)
         group(0, 2, PACK, HALF, HALF)
+        quantize_x(2, 0, HALF)
         sums2 = project(2, 0, HALF, (4, 5))
         for t in (2, 3):
             gather(1, t, HALF, HALF)
         group(1, 2, PACK, HALF, HALF)
+        quantize_x(0, HALF, HALF)
         sums0b = project(0, HALF, HALF, (6, 7))
         first_b = evacuate(sums0b, "first_b")
         for a in (HALF, HALF + P):
@@ -158,14 +181,18 @@ def tile_list_max_noneP_kernel(tc, xT, wgt, w, offs, out_0, out_1, out_2):
                 gather(2, t, a, P)
             group(2, 0, PACK, a, P)
         pool_two(best[0], sums1, first_a)
+        quantize_x(1, HALF, HALF)
         sums1b = project(1, HALF, HALF, (0, 1))
         y_a = pool_last(sums2, best[0], 0, HALF)
-        sums2b = [project(2, a, P, (bank,)) for a, bank in ((HALF, 2), (HALF + P, 3))]
+        sums2b = []
+        for a, bank in ((HALF, 2), (HALF + P, 3)):
+            quantize_x(2, a, P)
+            sums2b.append(project(2, a, P, (bank,)))
         pool_two(best[1], sums1b, first_b)
         y_b1 = pool_last(sums2b[0], best[1], HALF, P)
+        y_b2 = pool_last(sums2b[1], best[1], HALF + P, P)
         quantize_y(y_a, 0, HALF)
         nc.sync.dma_start(out=out_words[:, 0:HALF], in_=y_codes[:, 0:HALF].bitcast(I32))
-        y_b2 = pool_last(sums2b[1], best[1], HALF + P, P)
         quantize_y(y_b1, HALF, P)
         quantize_y(y_b2, HALF + P, P)
         nc.scalar.dma_start(out=out_words[:, HALF:J], in_=y_codes[:, HALF:J].bitcast(I32))

@@ -32,15 +32,14 @@ def tile_list_max_noneP_kernel(tc, xT, wgt, w, offs, out_0, out_1, out_2):
         factors = keep.tile([P, PICKS * J], F32, name="factors")
         early = [keep.tile([P, 2 * J], F32, name=f"early{c}") for c in range(2)]
         late_a = [keep.tile([P, (2 if c < 2 else PACK) * HALF], F32, name=f"late_a{c}", tag=f"late_a{c}", align_bytes=64) for c in range(PICKS)]
-        late_b = [keep.tile([P, (3, 2, 4)[c] * HALF], F32, name=f"late_b{c}", align_bytes=64) for c in range(PICKS)]
-        grouped_a = [late_b[c][:, (1, 0, 2)[c] * HALF :].bitcast(BF16) for c in range(PICKS)]
+        late_b = [keep.tile([P, (3, 3, 4)[c] * HALF], F32, name=f"late_b{c}", align_bytes=64) for c in range(PICKS)]
+        grouped_a = [late_b[c][:, (1, 1, 2)[c] * HALF :].bitcast(BF16) for c in range(PICKS)]
         grouped_b = [keep.tile([P, HALF * PACK], BF16, name=f"grouped_b{c}", align_bytes=64) for c in range(PICKS)]
         codes = [keep.tile([P, J], U32, name=f"codes{c}", align_bytes=64) for c in range(PICKS)]
         scales = [keep.tile([P, J], U8, name=f"scales{c}", align_bytes=64) for c in range(PICKS)]
         w_raw = keep.tile([P, PACK, N], F32, name="w_raw")
         w_grouped = keep.tile([P, N * PACK], BF16, name="w_grouped", align_bytes=64)
         w_scales = keep.tile([P, N], U8, name="w_scales", align_bytes=64)
-        y_codes = keep.tile([P, J], U32, name="y_codes", align_bytes=64)
         y_scales = keep.tile([P, J], U8, name="y_scales", align_bytes=64)
         x_rows = xT.rearrange("(p t) j -> p t j", t=PACK)
         out_rows = out_0.rearrange("(p t) j -> p t j", t=PACK)
@@ -92,49 +91,43 @@ def tile_list_max_noneP_kernel(tc, xT, wgt, w, offs, out_0, out_1, out_2):
         def quantize_x(c, a, n):
             quantize(codes[c][:, a : a + n], scales[c][:, a : a + n], grouped(c, a, n))
 
-        def project(c, a, n, banks):
-            per = BANK // n
-            sums = []
-            for s, bank in enumerate(banks):
-                acc = psum.tile([P, per, n], F32, name=f"sum_{c}_{a}_{s}", tag=f"bank{bank}")
-                for u in range(per):
-                    cols = slice(P * (s * per + u), P * (s * per + u + 1))
-                    nc.tensor.matmul_mx(
-                        out=acc[:, u, :],
-                        lhsT=w_codes[:, cols].bitcast(FP8X4),
-                        lhsT_scale=w_scales[:, cols],
-                        rhs=codes[c][:, a : a + n].bitcast(FP8X4),
-                        rhs_scale=scales[c][:, a : a + n],
-                        start=True,
-                        stop=True,
-                    )
-                sums.append(acc)
-            return sums
+        def project(c, q, bank):
+            acc = psum.tile([P, PACK, P], F32, name=f"sum_{c}_{q}", tag=f"bank{bank}")
+            places = slice(P * q, P * (q + 1))
+            for t in range(PACK):
+                cols = slice(P * t, P * (t + 1))
+                nc.tensor.matmul_mx(
+                    out=acc[:, t, :],
+                    lhsT=w_codes[:, cols].bitcast(FP8X4),
+                    lhsT_scale=w_scales[:, cols],
+                    rhs=codes[c][:, places].bitcast(FP8X4),
+                    rhs_scale=scales[c][:, places],
+                    start=True,
+                    stop=True,
+                )
+            return acc
 
-        def evacuate(sums, name):
-            tiles = []
-            for s, acc in enumerate(sums):
-                tile = keep.tile([P, 2, HALF], F32, name=f"{name}{s}")
-                nc.scalar.copy(out=tile[:], in_=acc[:])
-                tiles.append(tile)
-            return tiles
+        def evacuate(acc, q):
+            first = keep.tile([P, PACK, P], F32, name=f"first{q}")
+            nc.scalar.copy(out=first[:], in_=acc[:])
+            return first
 
-        def pool_two(best, sums, firsts):
-            for s, acc in enumerate(sums):
-                nc.vector.tensor_tensor(best[:, 2 * s : 2 * s + 2, :], acc[:], firsts[s][:], MAX)
+        def pool_two(acc, first, q):
+            best = keep.tile([P, PACK, P], F32, name=f"best{q}", tag=f"best{q}", align_bytes=64)
+            nc.vector.tensor_tensor(best[:], acc[:], first[:], MAX)
+            return best
 
-        def pool_last(sums, best, a, n):
-            per = BANK // n
-            y = keep.tile([P, PACK, n], F32, name=f"y{a}")
-            for s, acc in enumerate(sums):
-                nc.vector.tensor_tensor(y[:, s * per : (s + 1) * per, :], acc[:], best[:, s * per : (s + 1) * per, a % HALF : a % HALF + n], MAX)
+        def pool_last(y, acc, best):
+            nc.vector.tensor_tensor(y, acc[:], best[:], MAX)
+
+        def store_y(y, a, n):
             nc.sync.dma_start(out=out_rows[:, :, a : a + n], in_=y[:])
             y_grouped = keep.tile([P, n, PACK], BF16, name=f"y_grouped{a}", align_bytes=64)
             interleave(y_grouped[:], y[:])
             return y_grouped
 
-        def quantize_y(y_grouped, a, n):
-            quantize(y_codes[:, a : a + n], y_scales[:, a : a + n], y_grouped[:].rearrange("p j t -> p (j t)"))
+        def quantize_y(y_codes, y_grouped, a, n):
+            quantize(y_codes, y_scales[:, a : a + n], y_grouped[:].rearrange("p j t -> p (j t)"))
 
         gather(0, 0, 0, P)
         gather(0, 0, P, J - P)
@@ -153,49 +146,53 @@ def tile_list_max_noneP_kernel(tc, xT, wgt, w, offs, out_0, out_1, out_2):
         )
         for c in range(PICKS):
             gather(c, 2, 0, HALF)
-        gather(0, 2, HALF, HALF)
+        for c in range(2):
+            gather(c, 2, HALF, HALF)
         for c in range(PICKS):
             gather(c, 3, 0, HALF)
             group(c, 2 if c < 2 else 0, PACK, 0, HALF)
 
-        best = [keep.tile([P, PACK, HALF], F32, name=f"best{h}") for h in range(2)]
         quantize_x(0, 0, HALF)
         w_codes = keep.tile([P, N], U32, name="w_codes", tag="late_a0", align_bytes=64)
         quantize(w_codes[:], w_scales[:], w_grouped[:])
-        sums0 = project(0, 0, HALF, (0, 1))
-        first_a = evacuate(sums0, "first_a")
+        first = [evacuate(project(0, q, q), q) for q in (0, 1)]
         quantize_x(1, 0, HALF)
-        sums1 = project(1, 0, HALF, (2, 3))
+        sums1 = [project(1, q, 2 + q) for q in (0, 1)]
         gather(0, 3, HALF, HALF)
         group(0, 2, PACK, HALF, HALF)
         quantize_x(2, 0, HALF)
-        sums2 = project(2, 0, HALF, (4, 5))
-        for t in (2, 3):
-            gather(1, t, HALF, HALF)
+        sums2 = [project(2, q, 4 + q) for q in (0, 1)]
+        gather(1, 3, HALF, HALF)
         group(1, 2, PACK, HALF, HALF)
         quantize_x(0, HALF, HALF)
-        sums0b = project(0, HALF, HALF, (6, 7))
-        first_b = evacuate(sums0b, "first_b")
+        first.extend(evacuate(project(0, q, 4 + q), q) for q in (2, 3))
         for a in (HALF, HALF + P):
             for t in (2, 3):
                 gather(2, t, a, P)
             group(2, 0, PACK, a, P)
-        pool_two(best[0], sums1, first_a)
+        best = [pool_two(sums1[q], first[q], q) for q in (0, 1)]
         quantize_x(1, HALF, HALF)
-        sums1b = project(1, HALF, HALF, (0, 1))
-        y_a = pool_last(sums2, best[0], 0, HALF)
-        sums2b = []
-        for a, bank in ((HALF, 2), (HALF + P, 3)):
-            quantize_x(2, a, P)
-            sums2b.append(project(2, a, P, (bank,)))
-        pool_two(best[1], sums1b, first_b)
-        y_b1 = pool_last(sums2b[0], best[1], HALF, P)
-        y_b2 = pool_last(sums2b[1], best[1], HALF + P, P)
-        quantize_y(y_a, 0, HALF)
-        nc.sync.dma_start(out=out_words[:, 0:HALF], in_=y_codes[:, 0:HALF].bitcast(I32))
-        quantize_y(y_b1, HALF, P)
-        quantize_y(y_b2, HALF + P, P)
-        nc.scalar.dma_start(out=out_words[:, HALF:J], in_=y_codes[:, HALF:J].bitcast(I32))
+        sums1.extend(project(1, q, q - 2) for q in (2, 3))
+        y_a = keep.tile([P, PACK, HALF], F32, name="y_a")
+        for q in (0, 1):
+            pool_last(y_a[:, :, P * q : P * (q + 1)], sums2[q], best[q])
+        grouped_y_a = store_y(y_a, 0, HALF)
+        for q in (2, 3):
+            quantize_x(2, P * q, P)
+            sums2.append(project(2, q, q))
+        best.extend(pool_two(sums1[q], first[q], q) for q in (2, 3))
+        grouped_y_b = []
+        for q in (2, 3):
+            y_b = keep.tile([P, PACK, P], F32, name=f"y_b{q}")
+            pool_last(y_b[:], sums2[q], best[q])
+            grouped_y_b.append(store_y(y_b, P * q, P))
+        y_codes_a = keep.tile([P, HALF], U32, name="y_codes_a", tag="best2", align_bytes=64)
+        y_codes_b = keep.tile([P, HALF], U32, name="y_codes_b", align_bytes=64)
+        quantize_y(y_codes_a[:], grouped_y_a, 0, HALF)
+        nc.sync.dma_start(out=out_words[:, 0:HALF], in_=y_codes_a[:].bitcast(I32))
+        for q in (2, 3):
+            quantize_y(y_codes_b[:, P * (q - 2) : P * (q - 1)], grouped_y_b[q - 2], P * q, P)
+        nc.scalar.dma_start(out=out_words[:, HALF:J], in_=y_codes_b[:].bitcast(I32))
         for q in range(4):
             eng = nc.sync if q % 2 == 0 else nc.scalar
             eng.dma_start(out=out_2[0, 4 * q : 4 * q + 4, :].bitcast(I32), in_=y_scales[32 * q : 32 * q + 4, :].bitcast(I32))

@@ -19,6 +19,7 @@ P = 128
 PACK = 4
 BANK = 512
 HALF = J // 2
+LEAD = (2, 2, 1)
 
 
 def tile_list_max_noneP_kernel(tc, xT, wgt, w, offs, out_0, out_1, out_2):
@@ -29,11 +30,10 @@ def tile_list_max_noneP_kernel(tc, xT, wgt, w, offs, out_0, out_1, out_2):
 
         offsets = keep.tile([P, PICKS * J // 16], U16, name="offsets")
         planes = [keep.tile([P, T], F32, name=f"plane{t}") for t in range(PACK)]
-        factors = keep.tile([P, PICKS * J], F32, name="factors")
-        early = [keep.tile([P, 2 * J], F32, name=f"early{c}") for c in range(2)]
-        late_a = [keep.tile([P, (2 if c < 2 else PACK) * HALF], F32, name=f"late_a{c}", tag=f"late_a{c}", align_bytes=64) for c in range(PICKS)]
-        late_b = [keep.tile([P, (3, 3, 4)[c] * HALF], F32, name=f"late_b{c}", align_bytes=64) for c in range(PICKS)]
-        grouped_a = [late_b[c][:, (1, 1, 2)[c] * HALF :].bitcast(BF16) for c in range(PICKS)]
+        factors_head = keep.tile([P, HALF], F32, name="factors_head", tag="w_codes", align_bytes=64)
+        factors = keep.tile([P, PICKS * J - HALF], F32, name="factors")
+        late = [keep.tile([P, 4 * J + HALF], F32, name=f"late{c}", tag=f"late{c}", align_bytes=64) for c in range(PICKS)]
+        grouped_a = [late[c][:, 3 * J + HALF :].bitcast(BF16) for c in range(PICKS)]
         grouped_b = [keep.tile([P, HALF * PACK], BF16, name=f"grouped_b{c}", align_bytes=64) for c in range(PICKS)]
         codes = [keep.tile([P, J], U32, name=f"codes{c}", align_bytes=64) for c in range(PICKS)]
         scales = [keep.tile([P, J], U8, name=f"scales{c}", align_bytes=64) for c in range(PICKS)]
@@ -47,19 +47,16 @@ def tile_list_max_noneP_kernel(tc, xT, wgt, w, offs, out_0, out_1, out_2):
 
         nc.sync.dma_start(out=planes[0][:], in_=x_rows[:, 0, :])
         nc.sync.dma_start(offsets[:], offs)
-        for a, b in ((0, P), (P, J), (J, PICKS * J)):
-            nc.sync.dma_start(out=factors[:, a:b], in_=wgt[:, a:b])
+        nc.sync.dma_start(out=factors_head[:], in_=wgt[:, 0:HALF])
+        for a, b in ((HALF, J), (J, 2 * J), (2 * J, 3 * J)):
+            nc.sync.dma_start(out=factors[:, a - HALF : b - HALF], in_=wgt[:, a:b])
         nc.sync.dma_start(out=planes[1][:], in_=x_rows[:, 1, :])
         nc.sync.dma_start(out=planes[2][:], in_=x_rows[:, 2, :])
         nc.sync.dma_start(out=w_raw[:], in_=w.rearrange("(p t) n -> p t n", t=PACK))
         nc.sync.dma_start(out=planes[3][:], in_=x_rows[:, 3, :])
 
         def picked(c, t0, t1, a, n):
-            if c < 2 and t0 < 2:
-                return early[c][:].rearrange("p (t j) -> p t j", j=J)[:, t0:t1, a : a + n]
-            skip = 2 if c < 2 else 0
-            tile = late_a[c] if a < HALF else late_b[c]
-            return tile[:].rearrange("p (t j) -> p t j", j=HALF)[:, t0 - skip : t1 - skip, a % HALF : a % HALF + n]
+            return late[c][:, 0 : PACK * J].rearrange("p (t j) -> p t j", j=J)[:, t0:t1, a : a + n]
 
         def grouped(c, a, n):
             half = grouped_a[c] if a < HALF else grouped_b[c][:]
@@ -69,12 +66,12 @@ def tile_list_max_noneP_kernel(tc, xT, wgt, w, offs, out_0, out_1, out_2):
             nc.vector.tensor_tensor(
                 picked(c, t, t + 1, a, n)[:, 0, :],
                 planes[t][:].indirect(offsets[:, (c * J + a) // 16 : (c * J + a + n) // 16]),
-                factors[:, c * J + a : c * J + a + n],
+                factors_head[:] if c * J + a == 0 else factors[:, c * J + a - HALF : c * J + a - HALF + n],
                 MULT,
             )
 
-        def interleave(dst, src):
-            nc.scalar.copy(
+        def interleave(dst, src, copy=nc.scalar.copy):
+            copy(
                 out=dst.rearrange("p (c i) t -> p c t i", i=4),
                 in_=src.rearrange("p t (c i) -> p c t i", i=4),
             )
@@ -108,7 +105,7 @@ def tile_list_max_noneP_kernel(tc, xT, wgt, w, offs, out_0, out_1, out_2):
             return acc
 
         def evacuate(acc, q):
-            first = keep.tile([P, PACK, P], F32, name=f"first{q}")
+            first = keep.tile([P, PACK, P], F32, name=f"first{q}", tag=f"first{q}", align_bytes=64)
             nc.scalar.copy(out=first[:], in_=acc[:])
             return first
 
@@ -120,76 +117,68 @@ def tile_list_max_noneP_kernel(tc, xT, wgt, w, offs, out_0, out_1, out_2):
         def pool_last(y, acc, best):
             nc.vector.tensor_tensor(y, acc[:], best[:], MAX)
 
-        def store_y(y, a, n):
+        def store_y(y, a, n, slot, on_vector=0):
             nc.sync.dma_start(out=out_rows[:, :, a : a + n], in_=y[:])
-            y_grouped = keep.tile([P, n, PACK], BF16, name=f"y_grouped{a}", align_bytes=64)
-            interleave(y_grouped[:], y[:])
+            y_grouped = keep.tile([P, n, PACK], BF16, name=f"y_grouped{a}", tag=slot, align_bytes=64)
+            interleave(y_grouped[:, 0 : n - on_vector, :], y[:, :, 0 : n - on_vector])
             return y_grouped
 
         def quantize_y(y_codes, y_grouped, a, n):
             quantize(y_codes, y_scales[:, a : a + n], y_grouped[:].rearrange("p j t -> p (j t)"))
 
-        gather(0, 0, 0, P)
-        gather(0, 0, P, J - P)
-        gather(1, 0, 0, J)
-        gather(2, 0, 0, HALF)
-        gather(2, 0, HALF, HALF)
-        for c in range(2):
-            gather(c, 1, 0, J)
-            group(c, 0, 2, 0, HALF)
-            group(c, 0, 2, HALF, HALF)
-        gather(2, 1, 0, HALF)
-        gather(2, 1, HALF, HALF)
+        for t in range(PACK - 1):
+            for c in range(PICKS):
+                for a, n in ((0, HALF), (HALF, HALF)) if c == 0 else ((0, J),):
+                    gather(c, t, a, n)
+                if t + 1 == LEAD[c]:
+                    group(c, 0, LEAD[c], 0, HALF)
+                    group(c, 0, LEAD[c], HALF, HALF)
         nc.scalar.copy(
             out=w_grouped[:].rearrange("p (t m k) -> p m k t", t=PACK, k=PACK),
             in_=w_raw[:].rearrange("p k (m t) -> p m k t", t=PACK),
         )
         for c in range(PICKS):
-            gather(c, 2, 0, HALF)
-        for c in range(2):
-            gather(c, 2, HALF, HALF)
-        for c in range(PICKS):
             gather(c, 3, 0, HALF)
-            group(c, 2 if c < 2 else 0, PACK, 0, HALF)
+            group(c, LEAD[c], PACK, 0, HALF)
 
         quantize_x(0, 0, HALF)
-        w_codes = keep.tile([P, N], U32, name="w_codes", tag="late_a0", align_bytes=64)
+        w_codes = keep.tile([P, N], U32, name="w_codes", tag="w_codes", align_bytes=64)
         quantize(w_codes[:], w_scales[:], w_grouped[:])
         first = [evacuate(project(0, q, q), q) for q in (0, 1)]
         quantize_x(1, 0, HALF)
         sums1 = [project(1, q, 2 + q) for q in (0, 1)]
         gather(0, 3, HALF, HALF)
-        group(0, 2, PACK, HALF, HALF)
+        group(0, LEAD[0], PACK, HALF, HALF)
         quantize_x(2, 0, HALF)
         sums2 = [project(2, q, 4 + q) for q in (0, 1)]
         gather(1, 3, HALF, HALF)
-        group(1, 2, PACK, HALF, HALF)
+        group(1, LEAD[1], PACK, HALF, HALF)
         quantize_x(0, HALF, HALF)
         first.extend(evacuate(project(0, q, 4 + q), q) for q in (2, 3))
         for a in (HALF, HALF + P):
-            for t in (2, 3):
-                gather(2, t, a, P)
-            group(2, 0, PACK, a, P)
+            gather(2, 3, a, P)
+            group(2, LEAD[2], PACK, a, P)
         best = [pool_two(sums1[q], first[q], q) for q in (0, 1)]
         quantize_x(1, HALF, HALF)
         sums1.extend(project(1, q, q - 2) for q in (2, 3))
-        y_a = keep.tile([P, PACK, HALF], F32, name="y_a")
+        y_a = keep.tile([P, PACK, HALF], F32, name="y_a", tag="late1", align_bytes=64)
         for q in (0, 1):
             pool_last(y_a[:, :, P * q : P * (q + 1)], sums2[q], best[q])
-        grouped_y_a = store_y(y_a, 0, HALF)
         for q in (2, 3):
             quantize_x(2, P * q, P)
             sums2.append(project(2, q, q))
         best.extend(pool_two(sums1[q], first[q], q) for q in (2, 3))
+        grouped_y_a = store_y(y_a, 0, HALF, "first2")
         grouped_y_b = []
         for q in (2, 3):
             y_b = keep.tile([P, PACK, P], F32, name=f"y_b{q}")
             pool_last(y_b[:], sums2[q], best[q])
-            grouped_y_b.append(store_y(y_b, P * q, P))
+            grouped_y_b.append(store_y(y_b, P * q, P, f"y_grouped{q}", 64 if q == 3 else 0))
         y_codes_a = keep.tile([P, HALF], U32, name="y_codes_a", tag="best2", align_bytes=64)
         y_codes_b = keep.tile([P, HALF], U32, name="y_codes_b", align_bytes=64)
         quantize_y(y_codes_a[:], grouped_y_a, 0, HALF)
         nc.sync.dma_start(out=out_words[:, 0:HALF], in_=y_codes_a[:].bitcast(I32))
+        interleave(grouped_y_b[1][:, 64:P, :], y_b[:, :, 64:P], nc.vector.tensor_copy)
         for q in (2, 3):
             quantize_y(y_codes_b[:, P * (q - 2) : P * (q - 1)], grouped_y_b[q - 2], P * q, P)
         nc.scalar.dma_start(out=out_words[:, HALF:J], in_=y_codes_b[:].bitcast(I32))

from contextlib import ExitStack

import concourse.mybir as mybir

K, N, T, J, PICKS = 512, 512, 2048, 512, 3
FLOPS = 2 * K * N * J * PICKS

F32 = mybir.dt.float32
BF16 = mybir.dt.bfloat16
U32 = mybir.dt.uint32
I32 = mybir.dt.int32
U16 = mybir.dt.uint16
U8 = mybir.dt.uint8
FP8X4 = mybir.dt.float8_e4m3fn_x4
MULT = mybir.AluOpType.mult
MAX = mybir.AluOpType.max

P = 128
PACK = 4
BANK = 512
HALF = J // 2
LEAD = (2, 2, 1)


def tile_list_max_noneP_kernel(tc, xT, wgt, w, offs, out_0, out_1, out_2):
    nc = tc.nc
    with ExitStack() as ctx:
        keep = ctx.enter_context(tc.tile_pool(name="keep", bufs=1))
        psum = ctx.enter_context(tc.psum_pool(name="psum", bufs=1))

        offsets = keep.tile([P, PICKS * J // 16], U16, name="offsets")
        planes = [keep.tile([P, T], F32, name=f"plane{t}") for t in range(PACK)]
        factors_head = keep.tile([P, HALF], F32, name="factors_head", tag="w_codes", align_bytes=64)
        factors = keep.tile([P, PICKS * J - HALF], F32, name="factors")
        late = [keep.tile([P, 4 * J + HALF], F32, name=f"late{c}", tag=f"late{c}", align_bytes=64) for c in range(PICKS)]
        grouped_a = [late[c][:, 3 * J + HALF :].bitcast(BF16) for c in range(PICKS)]
        grouped_b = [keep.tile([P, HALF * PACK], BF16, name=f"grouped_b{c}", align_bytes=64) for c in range(PICKS)]
        codes = [keep.tile([P, J], U32, name=f"codes{c}", align_bytes=64) for c in range(PICKS)]
        scales = [keep.tile([P, J], U8, name=f"scales{c}", align_bytes=64) for c in range(PICKS)]
        w_raw = keep.tile([P, PACK, N], F32, name="w_raw")
        w_grouped = keep.tile([P, N * PACK], BF16, name="w_grouped", align_bytes=64)
        w_scales = keep.tile([P, N], U8, name="w_scales", align_bytes=64)
        y_scales = keep.tile([P, J], U8, name="y_scales", align_bytes=64)
        x_rows = xT.rearrange("(p t) j -> p t j", t=PACK)
        out_rows = out_0.rearrange("(p t) j -> p t j", t=PACK)
        out_words = out_1[0].rearrange("p j t -> p (j t)").bitcast(I32)

        nc.sync.dma_start(out=planes[0][:], in_=x_rows[:, 0, :])
        nc.sync.dma_start(offsets[:], offs)
        nc.sync.dma_start(out=factors_head[:], in_=wgt[:, 0:HALF])
        for a, b in ((HALF, J), (J, 2 * J), (2 * J, 3 * J)):
            nc.sync.dma_start(out=factors[:, a - HALF : b - HALF], in_=wgt[:, a:b])
        nc.sync.dma_start(out=planes[1][:], in_=x_rows[:, 1, :])
        nc.sync.dma_start(out=planes[2][:], in_=x_rows[:, 2, :])
        nc.sync.dma_start(out=w_raw[:], in_=w.rearrange("(p t) n -> p t n", t=PACK))
        nc.sync.dma_start(out=planes[3][:], in_=x_rows[:, 3, :])

        def picked(c, t0, t1, a, n):
            return late[c][:, 0 : PACK * J].rearrange("p (t j) -> p t j", j=J)[:, t0:t1, a : a + n]

        def grouped(c, a, n):
            half = grouped_a[c] if a < HALF else grouped_b[c][:]
            return half[:, PACK * (a % HALF) : PACK * (a % HALF + n)]

        def gather(c, t, a, n):
            nc.vector.tensor_tensor(
                picked(c, t, t + 1, a, n)[:, 0, :],
                planes[t][:].indirect(offsets[:, (c * J + a) // 16 : (c * J + a + n) // 16]),
                factors_head[:] if c * J + a == 0 else factors[:, c * J + a - HALF : c * J + a - HALF + n],
                MULT,
            )

        def interleave(dst, src, copy=nc.scalar.copy):
            copy(
                out=dst.rearrange("p (c i) t -> p c t i", i=4),
                in_=src.rearrange("p t (c i) -> p c t i", i=4),
            )

        def group(c, t0, t1, a, n):
            interleave(
                grouped(c, a, n).rearrange("p (j t) -> p j t", t=PACK)[:, :, t0:t1],
                picked(c, t0, t1, a, n),
            )

        def quantize(cod, sca, src):
            nc.vector.quantize_mx(out=cod.bitcast(FP8X4), scales=sca, in_=src)

        def quantize_x(c, a, n):
            quantize(codes[c][:, a : a + n], scales[c][:, a : a + n], grouped(c, a, n))

        def project(c, q, bank):
            acc = psum.tile([P, PACK, P], F32, name=f"sum_{c}_{q}", tag=f"bank{bank}")
            places = slice(P * q, P * (q + 1))
            for t in range(PACK):
                cols = slice(P * t, P * (t + 1))
                nc.tensor.matmul_mx(
                    out=acc[:, t, :],
                    lhsT=w_codes[:, cols].bitcast(FP8X4),
                    lhsT_scale=w_scales[:, cols],
                    rhs=codes[c][:, places].bitcast(FP8X4),
                    rhs_scale=scales[c][:, places],
                    start=True,
                    stop=True,
                )
            return acc

        def evacuate(acc, q):
            first = keep.tile([P, PACK, P], F32, name=f"first{q}", tag=f"first{q}", align_bytes=64)
            nc.scalar.copy(out=first[:], in_=acc[:])
            return first

        def pool_two(acc, first, q):
            best = keep.tile([P, PACK, P], F32, name=f"best{q}", tag=f"best{q}", align_bytes=64)
            nc.vector.tensor_tensor(best[:], acc[:], first[:], MAX)
            return best

        def pool_last(y, acc, best):
            nc.vector.tensor_tensor(y, acc[:], best[:], MAX)

        def store_y(y, a, n, slot, on_vector=0):
            nc.sync.dma_start(out=out_rows[:, :, a : a + n], in_=y[:])
            y_grouped = keep.tile([P, n, PACK], BF16, name=f"y_grouped{a}", tag=slot, align_bytes=64)
            interleave(y_grouped[:, 0 : n - on_vector, :], y[:, :, 0 : n - on_vector])
            return y_grouped

        def quantize_y(y_codes, y_grouped, a, n):
            quantize(y_codes, y_scales[:, a : a + n], y_grouped[:].rearrange("p j t -> p (j t)"))

        for t in range(PACK - 1):
            for c in range(PICKS):
                for a, n in ((0, HALF), (HALF, HALF)) if c == 0 else ((0, J),):
                    gather(c, t, a, n)
                if t + 1 == LEAD[c]:
                    group(c, 0, LEAD[c], 0, HALF)
                    group(c, 0, LEAD[c], HALF, HALF)
        nc.scalar.copy(
            out=w_grouped[:].rearrange("p (t m k) -> p m k t", t=PACK, k=PACK),
            in_=w_raw[:].rearrange("p k (m t) -> p m k t", t=PACK),
        )
        for c in range(PICKS):
            gather(c, 3, 0, HALF)
            group(c, LEAD[c], PACK, 0, HALF)

        quantize_x(0, 0, HALF)
        w_codes = keep.tile([P, N], U32, name="w_codes", tag="w_codes", align_bytes=64)
        quantize(w_codes[:], w_scales[:], w_grouped[:])
        first = [evacuate(project(0, q, q), q) for q in (0, 1)]
        quantize_x(1, 0, HALF)
        sums1 = [project(1, q, 2 + q) for q in (0, 1)]
        gather(0, 3, HALF, HALF)
        group(0, LEAD[0], PACK, HALF, HALF)
        quantize_x(2, 0, HALF)
        sums2 = [project(2, q, 4 + q) for q in (0, 1)]
        gather(1, 3, HALF, HALF)
        group(1, LEAD[1], PACK, HALF, HALF)
        quantize_x(0, HALF, HALF)
        first.extend(evacuate(project(0, q, 4 + q), q) for q in (2, 3))
        for a in (HALF, HALF + P):
            gather(2, 3, a, P)
            group(2, LEAD[2], PACK, a, P)
        best = [pool_two(sums1[q], first[q], q) for q in (0, 1)]
        quantize_x(1, HALF, HALF)
        sums1.extend(project(1, q, q - 2) for q in (2, 3))
        y_a = keep.tile([P, PACK, HALF], F32, name="y_a", tag="late1", align_bytes=64)
        for q in (0, 1):
            pool_last(y_a[:, :, P * q : P * (q + 1)], sums2[q], best[q])
        for q in (2, 3):
            quantize_x(2, P * q, P)
            sums2.append(project(2, q, q))
        best.extend(pool_two(sums1[q], first[q], q) for q in (2, 3))
        grouped_y_a = store_y(y_a, 0, HALF, "first2")
        grouped_y_b = []
        for q in (2, 3):
            y_b = keep.tile([P, PACK, P], F32, name=f"y_b{q}")
            pool_last(y_b[:], sums2[q], best[q])
            grouped_y_b.append(store_y(y_b, P * q, P, f"y_grouped{q}", 64 if q == 3 else 0))
        y_codes_a = keep.tile([P, HALF], U32, name="y_codes_a", tag="best2", align_bytes=64)
        y_codes_b = keep.tile([P, HALF], U32, name="y_codes_b", align_bytes=64)
        quantize_y(y_codes_a[:], grouped_y_a, 0, HALF)
        nc.sync.dma_start(out=out_words[:, 0:HALF], in_=y_codes_a[:].bitcast(I32))
        interleave(grouped_y_b[1][:, 64:P, :], y_b[:, :, 64:P], nc.vector.tensor_copy)
        for q in (2, 3):
            quantize_y(y_codes_b[:, P * (q - 2) : P * (q - 1)], grouped_y_b[q - 2], P * q, P)
        nc.scalar.dma_start(out=out_words[:, HALF:J], in_=y_codes_b[:].bitcast(I32))
        for q in range(4):
            eng = nc.sync if q % 2 == 0 else nc.scalar
            eng.dma_start(out=out_2[0, 4 * q : 4 * q + 4, :].bitcast(I32), in_=y_scales[32 * q : 32 * q + 4, :].bitcast(I32))
